import numpy as np
import ml_dtypes


def mxq(x, axis, fmt="e4m3"):
    dtype, down = {"e4m3": (ml_dtypes.float8_e4m3fn, 7), "e5m2": (ml_dtypes.float8_e5m2, 14)}[fmt]
    v = np.moveaxis(np.asarray(x, np.float32).astype(ml_dtypes.bfloat16).astype(np.float64), axis, -1)
    blocks = v.reshape(v.shape[:-1] + (-1, 32))
    amax = np.abs(blocks).max(-1, keepdims=True)
    byte = np.maximum(np.where(amax > 0, np.frexp(amax)[1] - 1 + 127, 0) - down, 1)
    scale = np.exp2(byte - 127.0)
    codes = (blocks / scale).astype(np.float32).astype(dtype).astype(np.float64)
    return np.moveaxis((codes * scale).reshape(v.shape), -1, axis)


WIDE = False


def mx_kscale(k):
    if not WIDE:
        return np.ones(k)
    levels = np.array([10, -10, 5, -5, 0])
    if k % 512:
        return np.exp2(np.random.permutation(np.resize(levels, k // 32))).repeat(32)
    a = np.empty((k // 512, 16))
    for p in range(k // 512):
        a[p, :8] = np.random.permutation(np.resize(levels, 8))
        for g in range(8):
            far = levels[np.abs(levels - a[p, g]) >= 10]
            a[p, g + 8] = far[np.random.randint(len(far))]
    return np.exp2(a.ravel()).repeat(32)


def f64(x):
    return np.asarray(x).astype(np.float64)


def striped(idx):
    return np.tile(idx.reshape(-1, 16).T, (8, 1)).astype(np.uint16)


def unstriped(offs):
    return offs[:16].T.reshape(-1).astype(np.int64)


def relu(v):
    return np.maximum(v, 0.0)


K, T, S, N = 512, 512, 512, 2048


def setup_inputs():
    n = np.random.standard_normal
    s = mx_kscale(K)[:, None]
    return {
        "w": (n((K, N)) / np.sqrt(K) / s).astype(np.float32),
        "xT": (n((K, T)) * s).astype(np.float32),
        "b": (0.3 * n((S, 1))).astype(np.float32),
        "offs": striped(np.sort(np.random.permutation(N)[:S])),
    }


def reference(w, xT, b, offs):
    idx = unstriped(offs)
    wq = mxq(f64(w)[:, idx], 0, "e4m3")
    return relu((wq.T @ mxq(f64(xT), 0, "e4m3")) + f64(b))

@@ -1,0 +1,119 @@
+from contextlib import ExitStack
+
+import concourse.mybir as mybir
+from concourse.masks import make_identity
+
+K, N, T, S = 512, 2048, 512, 512
+FLOPS = 2 * K * S * T
+
+F32 = mybir.dt.float32
+BF16 = mybir.dt.bfloat16
+U32 = mybir.dt.uint32
+U16 = mybir.dt.uint16
+U8 = mybir.dt.uint8
+FP8X4 = mybir.dt.float8_e4m3fn_x4
+ADD, MAX = mybir.AluOpType.add, mybir.AluOpType.max
+RELU = mybir.ActivationFunctionType.Relu
+
+P = 128
+PACK = 4
+H = 256
+FIRST = N - H
+
+
+def tile_picked_neuron_lin_relu_srt_e_kernel(tc, w, xT, b, offs, out):
+    nc = tc.nc
+    with ExitStack() as ctx:
+        keep = ctx.enter_context(tc.tile_pool(name="keep", bufs=1))
+        psum = ctx.enter_context(tc.psum_pool(name="psum", bufs=8))
+
+        w_rows = w.rearrange("(p j) n -> p j n", j=PACK)
+        x_rows = xT.rearrange("(p j) t -> p j t", j=PACK)
+
+        lists = keep.tile([P, S // 16], U16, name="lists")
+        planes = [keep.tile([P, N], F32, name="plane%d" % j) for j in range(PACK)]
+        x_raw = [keep.tile([P, PACK, H], F32, name="x_raw%d" % h) for h in range(2)]
+        b_rows = keep.tile([P, P], F32, name="b_rows")
+        ident = keep.tile([P, P], F32, name="ident")
+        bias = keep.tile([P, PACK], F32, name="bias")
+        warm = keep.tile([P, 1], F32, name="warm")
+
+        nc.vector.memset(b_rows[:], 0.0)
+        nc.vector.memset(warm[:], 0.0)
+        nc.scalar.activation(warm[:], warm[:], RELU)
+        nc.sync.dma_start(planes[0][:], w_rows[:, 0, :])
+        nc.sync.dma_start(lists[:], offs)
+        nc.sync.dma_start(b_rows[0:4, :], b.rearrange("(q m) o -> q (m o)", m=P))
+        nc.sync.dma_start(planes[1][:], w_rows[:, 1, :])
+        nc.sync.dma_start(planes[2][:], w_rows[:, 2, :])
+        nc.sync.dma_start(planes[3][:, 0:FIRST], w_rows[:, 3, 0:FIRST])
+        nc.sync.dma_start(planes[3][:, FIRST:N], w_rows[:, 3, FIRST:N])
+        for h in range(2):
+            nc.sync.dma_start(x_raw[h][:], x_rows[:, :, h * H : (h + 1) * H])
+
+        make_identity(nc, ident[:])
+        b_bank = psum.tile([P, P], F32, name="b_bank", tag="bank")
+        nc.tensor.transpose(b_bank[:], b_rows[:], ident[:])
+        nc.scalar.copy(bias[:], b_bank[:, 0:PACK])
+
+        picked = keep.tile([P, 2, S], F32, name="picked")
+        grouped = [keep.tile([P, H, PACK], BF16, name="grouped%d" % h, align_bytes=64) for h in range(2)]
+        codes = [keep.tile([P, H], U32, name="codes%d" % h, align_bytes=64) for h in range(2)]
+        scales = [keep.tile([P, H], U8, name="scales%d" % h, align_bytes=64) for h in range(2)]
+        x_grouped = [keep.tile([P, H, PACK], BF16, name="x_grouped%d" % h, align_bytes=64) for h in range(2)]
+        x_codes = [keep.tile([P, H], U32, name="x_codes%d" % h, align_bytes=64) for h in range(2)]
+        x_scales = [keep.tile([P, H], U8, name="x_scales%d" % h, align_bytes=64) for h in range(2)]
+
+        def weave(copy, h, j0):
+            cols = slice(h * H, (h + 1) * H)
+            copy(out=grouped[h][:, :, j0 : j0 + 2], in_=picked[:, j0 : j0 + 2, cols].rearrange("p j n -> p n j"))
+
+        def weave_x(copy, h, lo, hi):
+            copy(out=x_grouped[h][:, lo:hi, :], in_=x_raw[h][:, :, lo:hi].rearrange("p j n -> p n j"))
+
+        def quantise(codes_t, scales_t, grouped_t):
+            nc.vector.quantize_mx(
+                out=codes_t[:].bitcast(FP8X4), scales=scales_t[:], in_=grouped_t[:].rearrange("p n j -> p (n j)")
+            )
+
+        scrap = psum.tile([P, P], F32, name="scrap", tag="bank")
+        for j in range(2):
+            nc.vector.tensor_copy(picked[:, j, :], planes[j][:].indirect(lists[:]))
+        weave(nc.scalar.copy, 0, 0)
+        weave(nc.scalar.copy, 1, 0)
+        for h in range(2):
+            nc.vector.tensor_copy(grouped[h][:, :, 2], planes[2][:].indirect(lists[:, h * H // 16 : (h + 1) * H // 16]))
+        for i in range(16):
+            nc.tensor.transpose(scrap[:], planes[2][:, i * P : (i + 1) * P], ident[:])
+        nc.vector.tensor_copy(grouped[0][:, :, 3], planes[3][:, 0:FIRST].indirect(lists[:, 0 : H // 16]))
+        nc.vector.tensor_copy(grouped[1][:, :, 3], planes[3][:].indirect(lists[:, H // 16 : S // 16]))
+        for i in range(14):
+            nc.tensor.transpose(scrap[:], planes[3][:, i * P : (i + 1) * P], ident[:])
+        weave_x(nc.scalar.copy, 0, 0, H)
+        quantise(codes[0], scales[0], grouped[0])
+        quantise(codes[1], scales[1], grouped[1])
+        quantise(x_codes[0], x_scales[0], x_grouped[0])
+        weave_x(nc.scalar.copy, 1, 0, H // 2)
+        weave_x(nc.vector.tensor_copy, 1, H // 2, H)
+        quantise(x_codes[1], x_scales[1], x_grouped[1])
+
+        for h in range(2):
+            tokens = slice(h * H, (h + 1) * H)
+            for q in range(4):
+                cols = slice((q % 2) * P, (q % 2 + 1) * P)
+                acc = psum.tile([P, H], F32, name="acc", tag="bank")
+                nc.tensor.matmul_mx(
+                    out=acc[:],
+                    lhsT=codes[q // 2][:, cols].bitcast(FP8X4),
+                    lhsT_scale=scales[q // 2][:, cols],
+                    rhs=x_codes[h][:].bitcast(FP8X4),
+                    rhs_scale=x_scales[h][:],
+                    start=True,
+                    stop=True,
+                )
+                result = keep.tile([P, H], F32, name="result%d%d" % (h, q))
+                if q % 2 == 0:
+                    nc.scalar.activation(result[:], acc[:], RELU, bias=bias[:, q : q + 1])
+                else:
+                    nc.vector.tensor_scalar(result[:], acc[:], bias[:, q : q + 1], 0.0, op0=ADD, op1=MAX)
+                nc.sync.dma_start(out[q * P : (q + 1) * P, tokens], result[:])

@@ -32,7 +32,7 @@ def tile_picked_neuron_lin_relu_srt_e_kernel(tc, w, xT, b, offs, out):
 
         lists = keep.tile([P, S // 16], U16, name="lists")
         planes = [keep.tile([P, N], F32, name="plane%d" % j) for j in range(PACK)]
-        x_raw = [keep.tile([P, PACK, H], F32, name="x_raw%d" % h) for h in range(2)]
+        x_raw = [keep.tile([P, PACK, T], F32, name="x_raw%d" % h) for h in range(1)]
         b_rows = keep.tile([P, P], F32, name="b_rows")
         ident = keep.tile([P, P], F32, name="ident")
         bias = keep.tile([P, PACK], F32, name="bias")
@@ -41,15 +41,14 @@ def tile_picked_neuron_lin_relu_srt_e_kernel(tc, w, xT, b, offs, out):
         nc.vector.memset(b_rows[:], 0.0)
         nc.vector.memset(warm[:], 0.0)
         nc.scalar.activation(warm[:], warm[:], RELU)
-        nc.sync.dma_start(planes[0][:], w_rows[:, 0, :])
+        nc.sync.dma_start(x_raw[0][:], x_rows)
         nc.sync.dma_start(lists[:], offs)
         nc.sync.dma_start(b_rows[0:4, :], b.rearrange("(q m) o -> q (m o)", m=P))
+        nc.sync.dma_start(planes[0][:], w_rows[:, 0, :])
         nc.sync.dma_start(planes[1][:], w_rows[:, 1, :])
         nc.sync.dma_start(planes[2][:], w_rows[:, 2, :])
         nc.sync.dma_start(planes[3][:, 0:FIRST], w_rows[:, 3, 0:FIRST])
         nc.sync.dma_start(planes[3][:, FIRST:N], w_rows[:, 3, FIRST:N])
-        for h in range(2):
-            nc.sync.dma_start(x_raw[h][:], x_rows[:, :, h * H : (h + 1) * H])
 
         make_identity(nc, ident[:])
         b_bank = psum.tile([P, P], F32, name="b_bank", tag="bank")
@@ -60,60 +59,79 @@ def tile_picked_neuron_lin_relu_srt_e_kernel(tc, w, xT, b, offs, out):
         grouped = [keep.tile([P, H, PACK], BF16, name="grouped%d" % h, align_bytes=64) for h in range(2)]
         codes = [keep.tile([P, H], U32, name="codes%d" % h, align_bytes=64) for h in range(2)]
         scales = [keep.tile([P, H], U8, name="scales%d" % h, align_bytes=64) for h in range(2)]
-        x_grouped = [keep.tile([P, H, PACK], BF16, name="x_grouped%d" % h, align_bytes=64) for h in range(2)]
-        x_codes = [keep.tile([P, H], U32, name="x_codes%d" % h, align_bytes=64) for h in range(2)]
-        x_scales = [keep.tile([P, H], U8, name="x_scales%d" % h, align_bytes=64) for h in range(2)]
+        x_grouped = keep.tile([P, T, PACK], BF16, name="x_grouped", align_bytes=64)
+        x_codes = keep.tile([P, T], U32, name="x_codes", align_bytes=64)
+        x_scales = keep.tile([P, T], U8, name="x_scales", align_bytes=64)
 
         def weave(copy, h, j0):
             cols = slice(h * H, (h + 1) * H)
             copy(out=grouped[h][:, :, j0 : j0 + 2], in_=picked[:, j0 : j0 + 2, cols].rearrange("p j n -> p n j"))
 
         def weave_x(copy, h, lo, hi):
-            copy(out=x_grouped[h][:, lo:hi, :], in_=x_raw[h][:, :, lo:hi].rearrange("p j n -> p n j"))
+            copy(out=x_grouped[:, h * H + lo : h * H + hi, :], in_=x_raw[h][:, :, lo:hi].rearrange("p j n -> p n j"))
 
         def quantise(codes_t, scales_t, grouped_t):
             nc.vector.quantize_mx(
-                out=codes_t[:].bitcast(FP8X4), scales=scales_t[:], in_=grouped_t[:].rearrange("p n j -> p (n j)")
+                out=codes_t.bitcast(FP8X4), scales=scales_t, in_=grouped_t.rearrange("p n j -> p (n j)")
             )
 
+        def quantise_x(lo, hi):
+            quantise(x_codes[:, lo:hi], x_scales[:, lo:hi], x_grouped[:, lo:hi, :])
+
+        def quantise_w(h):
+            quantise(codes[h][:], scales[h][:], grouped[h][:])
+
+        def multiply(q, lo, hi):
+            acc = psum.tile([P, hi - lo], F32, name="acc", tag="bank")
+            cols = slice((q % 2) * P, (q % 2 + 1) * P)
+            nc.tensor.matmul_mx(
+                out=acc[:],
+                lhsT=codes[q // 2][:, cols].bitcast(FP8X4),
+                lhsT_scale=scales[q // 2][:, cols],
+                rhs=x_codes[:, lo:hi].bitcast(FP8X4),
+                rhs_scale=x_scales[:, lo:hi],
+                start=True,
+                stop=True,
+            )
+            return acc
+
+        results = [keep.tile([P, T], F32, name="result%d" % q) for q in range(4)]
+
+        def finish_scalar(acc, q, lo, hi):
+            nc.scalar.activation(results[q][:, lo:hi], acc[:], RELU, bias=bias[:, q : q + 1])
+
+        def finish_vector(acc, q, lo, hi):
+            nc.vector.tensor_scalar(results[q][:, lo:hi], acc[:], bias[:, q : q + 1], 0.0, op0=ADD, op1=MAX)
+
+        def store(q):
+            nc.sync.dma_start(out[q * P : (q + 1) * P, :], results[q][:])
+
         scrap = psum.tile([P, P], F32, name="scrap", tag="bank")
+
+        def exercise(j, count):
+            for i in range(count):
+                nc.tensor.transpose(scrap[:], planes[j][:, i * P : (i + 1) * P], ident[:])
+
+        weave_x(nc.scalar.copy, 0, 0, T)
+        quantise_x(0, T)
         for j in range(2):
             nc.vector.tensor_copy(picked[:, j, :], planes[j][:].indirect(lists[:]))
         weave(nc.scalar.copy, 0, 0)
         weave(nc.scalar.copy, 1, 0)
         for h in range(2):
             nc.vector.tensor_copy(grouped[h][:, :, 2], planes[2][:].indirect(lists[:, h * H // 16 : (h + 1) * H // 16]))
-        for i in range(16):
-            nc.tensor.transpose(scrap[:], planes[2][:, i * P : (i + 1) * P], ident[:])
+        exercise(2, 16)
         nc.vector.tensor_copy(grouped[0][:, :, 3], planes[3][:, 0:FIRST].indirect(lists[:, 0 : H // 16]))
         nc.vector.tensor_copy(grouped[1][:, :, 3], planes[3][:].indirect(lists[:, H // 16 : S // 16]))
-        for i in range(14):
-            nc.tensor.transpose(scrap[:], planes[3][:, i * P : (i + 1) * P], ident[:])
-        weave_x(nc.scalar.copy, 0, 0, H)
-        quantise(codes[0], scales[0], grouped[0])
-        quantise(codes[1], scales[1], grouped[1])
-        quantise(x_codes[0], x_scales[0], x_grouped[0])
-        weave_x(nc.scalar.copy, 1, 0, H // 2)
-        weave_x(nc.vector.tensor_copy, 1, H // 2, H)
-        quantise(x_codes[1], x_scales[1], x_grouped[1])
-
-        for h in range(2):
-            tokens = slice(h * H, (h + 1) * H)
-            for q in range(4):
-                cols = slice((q % 2) * P, (q % 2 + 1) * P)
-                acc = psum.tile([P, H], F32, name="acc", tag="bank")
-                nc.tensor.matmul_mx(
-                    out=acc[:],
-                    lhsT=codes[q // 2][:, cols].bitcast(FP8X4),
-                    lhsT_scale=scales[q // 2][:, cols],
-                    rhs=x_codes[h][:].bitcast(FP8X4),
-                    rhs_scale=x_scales[h][:],
-                    start=True,
-                    stop=True,
-                )
-                result = keep.tile([P, H], F32, name="result%d%d" % (h, q))
-                if q % 2 == 0:
-                    nc.scalar.activation(result[:], acc[:], RELU, bias=bias[:, q : q + 1])
-                else:
-                    nc.vector.tensor_scalar(result[:], acc[:], bias[:, q : q + 1], 0.0, op0=ADD, op1=MAX)
-                nc.sync.dma_start(out[q * P : (q + 1) * P, tokens], result[:])
+        exercise(3, 8)
+        quantise_w(0)
+        for q in range(2):
+            acc = multiply(q, 0, T)
+            finish_scalar(acc, q, 0, T)
+            store(q)
+        quantise_w(1)
+        for q in range(2, 4):
+            for h in range(2):
+                acc = multiply(q, h * H, (h + 1) * H)
+                (finish_scalar, finish_vector)[h](acc, q, h * H, (h + 1) * H)
+            store(q)

@@ -68,7 +68,7 @@ def tile_picked_neuron_lin_relu_srt_e_kernel(tc, w, xT, b, offs, out):
             copy(out=grouped[h][:, :, j0 : j0 + 2], in_=picked[:, j0 : j0 + 2, cols].rearrange("p j n -> p n j"))
 
         def weave_x(copy, h, lo, hi):
-            copy(out=x_grouped[:, h * H + lo : h * H + hi, :], in_=x_raw[h][:, :, lo:hi].rearrange("p j n -> p n j"))
+            copy(out=x_grouped[:, lo:hi, :], in_=x_raw[h][:, :, lo:hi].rearrange("p j n -> p n j"))
 
         def quantise(codes_t, scales_t, grouped_t):
             nc.vector.quantize_mx(
@@ -122,15 +122,15 @@ def tile_picked_neuron_lin_relu_srt_e_kernel(tc, w, xT, b, offs, out):
             nc.vector.tensor_copy(grouped[h][:, :, 2], planes[2][:].indirect(lists[:, h * H // 16 : (h + 1) * H // 16]))
         exercise(2, 16)
         nc.vector.tensor_copy(grouped[0][:, :, 3], planes[3][:, 0:FIRST].indirect(lists[:, 0 : H // 16]))
-        nc.vector.tensor_copy(grouped[1][:, :, 3], planes[3][:].indirect(lists[:, H // 16 : S // 16]))
-        exercise(3, 8)
+        exercise(3, 6)
         quantise_w(0)
-        for q in range(2):
-            acc = multiply(q, 0, T)
-            finish_scalar(acc, q, 0, T)
-            store(q)
+        for h in range(2):
+            acc = multiply(0, h * H, (h + 1) * H)
+            finish_scalar(acc, 0, h * H, (h + 1) * H)
+            nc.sync.dma_start(out[0:P, h * H : (h + 1) * H], results[0][:, h * H : (h + 1) * H])
+        nc.vector.tensor_copy(grouped[1][:, :, 3], planes[3][:].indirect(lists[:, H // 16 : S // 16]))
         quantise_w(1)
-        for q in range(2, 4):
+        for q in range(1, 4):
             for h in range(2):
                 acc = multiply(q, h * H, (h + 1) * H)
                 (finish_scalar, finish_vector)[h](acc, q, h * H, (h + 1) * H)

from contextlib import ExitStack

import concourse.mybir as mybir
from concourse.masks import make_identity

K, N, T, S = 512, 2048, 512, 512
FLOPS = 2 * K * S * T

F32 = mybir.dt.float32
BF16 = mybir.dt.bfloat16
U32 = mybir.dt.uint32
U16 = mybir.dt.uint16
U8 = mybir.dt.uint8
FP8X4 = mybir.dt.float8_e4m3fn_x4
ADD, MAX = mybir.AluOpType.add, mybir.AluOpType.max
RELU = mybir.ActivationFunctionType.Relu

P = 128
PACK = 4
H = 256
FIRST = N - H


def tile_picked_neuron_lin_relu_srt_e_kernel(tc, w, xT, b, offs, out):
    nc = tc.nc
    with ExitStack() as ctx:
        keep = ctx.enter_context(tc.tile_pool(name="keep", bufs=1))
        psum = ctx.enter_context(tc.psum_pool(name="psum", bufs=8))

        w_rows = w.rearrange("(p j) n -> p j n", j=PACK)
        x_rows = xT.rearrange("(p j) t -> p j t", j=PACK)

        lists = keep.tile([P, S // 16], U16, name="lists")
        planes = [keep.tile([P, N], F32, name="plane%d" % j) for j in range(PACK)]
        x_raw = [keep.tile([P, PACK, T], F32, name="x_raw%d" % h) for h in range(1)]
        b_rows = keep.tile([P, P], F32, name="b_rows")
        ident = keep.tile([P, P], F32, name="ident")
        bias = keep.tile([P, PACK], F32, name="bias")
        warm = keep.tile([P, 1], F32, name="warm")

        nc.vector.memset(b_rows[:], 0.0)
        nc.vector.memset(warm[:], 0.0)
        nc.scalar.activation(warm[:], warm[:], RELU)
        nc.sync.dma_start(x_raw[0][:], x_rows)
        nc.sync.dma_start(lists[:], offs)
        nc.sync.dma_start(b_rows[0:4, :], b.rearrange("(q m) o -> q (m o)", m=P))
        nc.sync.dma_start(planes[0][:], w_rows[:, 0, :])
        nc.sync.dma_start(planes[1][:], w_rows[:, 1, :])
        nc.sync.dma_start(planes[2][:], w_rows[:, 2, :])
        nc.sync.dma_start(planes[3][:, 0:FIRST], w_rows[:, 3, 0:FIRST])
        nc.sync.dma_start(planes[3][:, FIRST:N], w_rows[:, 3, FIRST:N])

        make_identity(nc, ident[:])
        b_bank = psum.tile([P, P], F32, name="b_bank", tag="bank")
        nc.tensor.transpose(b_bank[:], b_rows[:], ident[:])
        nc.scalar.copy(bias[:], b_bank[:, 0:PACK])

        picked = keep.tile([P, 2, S], F32, name="picked")
        grouped = [keep.tile([P, H, PACK], BF16, name="grouped%d" % h, align_bytes=64) for h in range(2)]
        codes = [keep.tile([P, H], U32, name="codes%d" % h, align_bytes=64) for h in range(2)]
        scales = [keep.tile([P, H], U8, name="scales%d" % h, align_bytes=64) for h in range(2)]
        x_grouped = keep.tile([P, T, PACK], BF16, name="x_grouped", align_bytes=64)
        x_codes = keep.tile([P, T], U32, name="x_codes", align_bytes=64)
        x_scales = keep.tile([P, T], U8, name="x_scales", align_bytes=64)

        def weave(copy, h, j0):
            cols = slice(h * H, (h + 1) * H)
            copy(out=grouped[h][:, :, j0 : j0 + 2], in_=picked[:, j0 : j0 + 2, cols].rearrange("p j n -> p n j"))

        def weave_x(copy, h, lo, hi):
            copy(out=x_grouped[:, lo:hi, :], in_=x_raw[h][:, :, lo:hi].rearrange("p j n -> p n j"))

        def quantise(codes_t, scales_t, grouped_t):
            nc.vector.quantize_mx(
                out=codes_t.bitcast(FP8X4), scales=scales_t, in_=grouped_t.rearrange("p n j -> p (n j)")
            )

        def quantise_x(lo, hi):
            quantise(x_codes[:, lo:hi], x_scales[:, lo:hi], x_grouped[:, lo:hi, :])

        def quantise_w(h):
            quantise(codes[h][:], scales[h][:], grouped[h][:])

        def multiply(q, lo, hi):
            acc = psum.tile([P, hi - lo], F32, name="acc", tag="bank")
            cols = slice((q % 2) * P, (q % 2 + 1) * P)
            nc.tensor.matmul_mx(
                out=acc[:],
                lhsT=codes[q // 2][:, cols].bitcast(FP8X4),
                lhsT_scale=scales[q // 2][:, cols],
                rhs=x_codes[:, lo:hi].bitcast(FP8X4),
                rhs_scale=x_scales[:, lo:hi],
                start=True,
                stop=True,
            )
            return acc

        results = [keep.tile([P, T], F32, name="result%d" % q) for q in range(4)]

        def finish_scalar(acc, q, lo, hi):
            nc.scalar.activation(results[q][:, lo:hi], acc[:], RELU, bias=bias[:, q : q + 1])

        def finish_vector(acc, q, lo, hi):
            nc.vector.tensor_scalar(results[q][:, lo:hi], acc[:], bias[:, q : q + 1], 0.0, op0=ADD, op1=MAX)

        def store(q):
            nc.sync.dma_start(out[q * P : (q + 1) * P, :], results[q][:])

        scrap = psum.tile([P, P], F32, name="scrap", tag="bank")

        def exercise(j, count):
            for i in range(count):
                nc.tensor.transpose(scrap[:], planes[j][:, i * P : (i + 1) * P], ident[:])

        weave_x(nc.scalar.copy, 0, 0, T)
        quantise_x(0, T)
        for j in range(2):
            nc.vector.tensor_copy(picked[:, j, :], planes[j][:].indirect(lists[:]))
        weave(nc.scalar.copy, 0, 0)
        weave(nc.scalar.copy, 1, 0)
        for h in range(2):
            nc.vector.tensor_copy(grouped[h][:, :, 2], planes[2][:].indirect(lists[:, h * H // 16 : (h + 1) * H // 16]))
        exercise(2, 16)
        nc.vector.tensor_copy(grouped[0][:, :, 3], planes[3][:, 0:FIRST].indirect(lists[:, 0 : H // 16]))
        exercise(3, 6)
        quantise_w(0)
        for h in range(2):
            acc = multiply(0, h * H, (h + 1) * H)
            finish_scalar(acc, 0, h * H, (h + 1) * H)
            nc.sync.dma_start(out[0:P, h * H : (h + 1) * H], results[0][:, h * H : (h + 1) * H])
        nc.vector.tensor_copy(grouped[1][:, :, 3], planes[3][:].indirect(lists[:, H // 16 : S // 16]))
        quantise_w(1)
        for q in range(1, 4):
            for h in range(2):
                acc = multiply(q, h * H, (h + 1) * H)
                (finish_scalar, finish_vector)[h](acc, q, h * H, (h + 1) * H)
            store(q)
